import numpy as np
import ml_dtypes


def mxq(x, axis, fmt="e4m3"):
    dtype, down = {"e4m3": (ml_dtypes.float8_e4m3fn, 7), "e5m2": (ml_dtypes.float8_e5m2, 14)}[fmt]
    v = np.moveaxis(np.asarray(x, np.float32).astype(ml_dtypes.bfloat16).astype(np.float64), axis, -1)
    blocks = v.reshape(v.shape[:-1] + (-1, 32))
    amax = np.abs(blocks).max(-1, keepdims=True)
    byte = np.maximum(np.where(amax > 0, np.frexp(amax)[1] - 1 + 127, 0) - down, 1)
    scale = np.exp2(byte - 127.0)
    codes = (blocks / scale).astype(np.float32).astype(dtype).astype(np.float64)
    return np.moveaxis((codes * scale).reshape(v.shape), -1, axis)


WIDE = False


def mx_kscale(k):
    if not WIDE:
        return np.ones(k)
    levels = np.array([10, -10, 5, -5, 0])
    if k % 512:
        return np.exp2(np.random.permutation(np.resize(levels, k // 32))).repeat(32)
    a = np.empty((k // 512, 16))
    for p in range(k // 512):
        a[p, :8] = np.random.permutation(np.resize(levels, 8))
        for g in range(8):
            far = levels[np.abs(levels - a[p, g]) >= 10]
            a[p, g + 8] = far[np.random.randint(len(far))]
    return np.exp2(a.ravel()).repeat(32)


def f64(x):
    return np.asarray(x).astype(np.float64)


def striped(idx):
    return np.tile(idx.reshape(-1, 16).T, (8, 1)).astype(np.uint16)


def unstriped(offs):
    return offs[:16].T.reshape(-1).astype(np.int64)


def striped8(idx):
    return np.concatenate([x.reshape(-1, 16).T for x in idx]).astype(np.uint16)


def runs(offs, k):
    lists = np.stack([offs[16 * r : 16 * r + 16].T.reshape(-1) for r in range(8)]).astype(np.int64)
    return lists[np.arange(k) % 512 // 64]


def pack_weight(w):
    k, n = w.shape
    w = f64(np.asarray(w, np.float32).astype(ml_dtypes.bfloat16)).reshape(k // 32, 32, n)
    amax = np.abs(w).max(1)
    byte = np.clip(np.where(amax > 0, np.frexp(amax)[1] - 1 + 127 - 7, 1), 1, 254)
    scaled = (w * np.exp2(127.0 - byte)[:, None, :]).reshape(k, n).astype(np.float32)
    words = np.ascontiguousarray(scaled.reshape(k // 512, 128, 4, n).transpose(0, 1, 3, 2)).astype(ml_dtypes.float8_e4m3fn).view(np.uint8)
    return words, np.ascontiguousarray(byte.astype(np.uint8).reshape(k // 512, 16, n))


def unpack_weight(words, scales):
    g, p, n, _ = words.shape
    vals = np.ascontiguousarray(words).view(ml_dtypes.float8_e4m3fn).astype(np.float64) * np.repeat(np.exp2(scales.astype(np.float64) - 127.0), 8, axis=1)[..., None]
    return vals.transpose(0, 1, 3, 2).reshape(g * 512, n)


def sigmoid(v):
    return 1.0 / (1.0 + np.exp(-np.maximum(v, -700.0)))


K, T, S, N, H, J = 512, 2048, 512, 512, 512, 512


def setup_inputs():
    n = np.random.standard_normal
    s = mx_kscale(K)[:, None]
    u = mx_kscale(S)
    packed_xT = pack_weight(n((K, T)) * s)
    return {
        "x_words": packed_xT[0],
        "x_scales": packed_xT[1],
        "wa": (n((K, H)) / np.sqrt(K) / s).astype(np.float32),
        "tab": n((S, J)).astype(np.float32),
        "gt": (np.random.uniform(0.5, 1.5, (S, 1)) * u[:, None]).astype(np.float32),
        "w1": (n((S, N)) / np.sqrt(S) / u[:, None]).astype(np.float32),
        "offs": striped(np.random.permutation(T)[:S]),
        "n1": striped8(np.random.randint(0, J, (8, H))),
        "n2": striped8(np.stack([np.random.permutation(H) for _ in range(8)])),
        "n3": striped8(np.stack([np.random.permutation(H) for _ in range(8)])),
    }


def reference(x_words, x_scales, wa, tab, gt, w1, offs, n1, n2, n3):
    xq = unpack_weight(x_words, x_scales)[:, unstriped(offs)]
    y = xq.T @ mxq(f64(wa), 0, "e4m3")
    z = f64(gt) * (np.abs(y - (y[np.arange(S)[:, None], runs(n2, S)]) - (f64(tab)[np.arange(S)[:, None], runs(n1, S)])))
    h = mxq(f64(w1), 0, "e4m3").T @ mxq(z, 0, "e4m3")
    st = h * (sigmoid(h[np.arange(N)[:, None], runs(n3, N)]))
    return np.maximum(st, st[np.arange(N)[:, None], runs(n3, N)])

@@ -1,0 +1,220 @@
+from contextlib import ExitStack
+
+import concourse.mybir as mybir
+
+K, T, S, N, H = 512, 2048, 512, 512, 512
+FLOPS = 2 * K * S * H + 2 * S * N * H
+
+F32 = mybir.dt.float32
+BF16 = mybir.dt.bfloat16
+I32 = mybir.dt.int32
+U32 = mybir.dt.uint32
+U16 = mybir.dt.uint16
+U8 = mybir.dt.uint8
+FP8X4 = mybir.dt.float8_e4m3fn_x4
+ALU = mybir.AluOpType
+ACT = mybir.ActivationFunctionType
+
+P = 128
+PACK = 4
+HALF = 256
+CHUNKS = [(0, 256), (256, 512)]
+
+
+def tile_picked_tokkinddtwicp_none_p_kernel(tc, x_words, x_scales, wa, tab, gt, w1, offs, n1, n2, n3, out):
+    nc = tc.nc
+    with ExitStack() as ctx:
+        held = ctx.enter_context(tc.tile_pool(name="held", bufs=1))
+        psum = ctx.enter_context(tc.psum_pool(name="psum", bufs=8))
+
+        def keep(shape, dtype, name, tag=None):
+            return held.tile(shape, dtype, name=name, tag=tag or name, align_bytes=64)
+
+        def entries(lst, c0, c1):
+            return lst[:, c0 // 16 : c1 // 16]
+
+        offs_sb = keep([P, 32], U16, "offs_sb")
+        n1_sb = keep([P, 32], U16, "n1_sb")
+        n2_sb = keep([P, 32], U16, "n2_sb")
+        n3_sb = keep([P, 32], U16, "n3_sb")
+        words_all = keep([P, T], I32, "words_all")
+        scales_all = keep([P, T], U8, "scales_all")
+        nc.vector.memset(scales_all[:].bitcast(I32), 0)
+
+        warm = keep([P, 8], F32, "warm")
+        nc.gpsimd.memset(warm[:], 0.0)
+        warm2 = keep([P, 8], F32, "warm2")
+        nc.scalar.activation(warm2[:], warm[:], ACT.Sigmoid)
+
+        words_hbm = x_words[0].rearrange("p n t -> p (n t)").bitcast(I32)
+        nc.sync.dma_start(offs_sb[:], offs)
+        nc.sync.dma_start(words_all[:, 0 : T // 2], words_hbm[:, 0 : T // 2])
+        for q in range(4):
+            nc.sync.dma_start(scales_all[32 * q : 32 * q + 4, :].bitcast(I32), x_scales[0, 4 * q : 4 * q + 4, :].bitcast(I32))
+        nc.sync.dma_start(words_all[:, T // 2 : T], words_hbm[:, T // 2 : T])
+        wa_rows = wa.rearrange("(p j) n -> p j n", j=PACK)
+        wa_raw = [keep([P, PACK, HALF], F32, "wa_raw%d" % h) for h in range(2)]
+        for h in range(2):
+            nc.sync.dma_start(wa_raw[h][:], wa_rows[:, :, h * HALF : (h + 1) * HALF])
+        nc.sync.dma_start(n1_sb[:], n1)
+        tab_rows = tab.rearrange("(p t) n -> p t n", t=PACK)
+        tab_sb = [keep([P, H], F32, "tab%d" % t) for t in range(PACK)]
+        for t in range(PACK):
+            nc.sync.dma_start(tab_sb[t][:], tab_rows[:, t, :])
+        nc.sync.dma_start(n2_sb[:], n2)
+        gt_sb = keep([P, PACK], F32, "gt_sb")
+        nc.sync.dma_start(gt_sb[:], gt.rearrange("(p t) o -> p (t o)", t=PACK))
+        w1_rows = w1.rearrange("(p j) n -> p j n", j=PACK)
+        w1_raw = [keep([P, 2, N], F32, "w1_raw%d" % u) for u in range(2)]
+        for u in range(2):
+            nc.sync.dma_start(w1_raw[u][:], w1_rows[:, 2 * u : 2 * u + 2, :])
+        nc.sync.dma_start(n3_sb[:], n3)
+
+        scales_got = keep([P, S], U8, "scales_got")
+        nc.vector.tensor_copy(scales_got[:], scales_all[:].indirect(offs_sb[:]))
+        x_codes = keep([P, S], U32, "x_codes")
+        nc.vector.tensor_copy(x_codes[:].rearrange("p (t m) -> p m t", t=PACK), words_all[:].bitcast(U32).indirect(offs_sb[:]))
+        x_plane = keep([P, S], U8, "x_plane")
+        nc.vector.tensor_copy(x_plane[:].rearrange("p (t m) -> p t m", t=PACK), scales_got[:].rearrange("p (m t) -> p t m", t=PACK))
+
+        y = [keep([P, H], F32, "y%d" % t) for t in range(PACK)]
+        for h in range(2):
+            wa_bf = keep([P, HALF, PACK], BF16, "wa_bf%d" % h)
+            dst = wa_bf[:].rearrange("p (c i) j -> p c j i", i=4)
+            src = wa_raw[h][:].rearrange("p j (c i) -> p c j i", i=4)
+            if h == 0:
+                nc.scalar.copy(dst, src)
+            else:
+                nc.vector.tensor_copy(dst[:, 0:40], src[:, 0:40])
+                nc.scalar.copy(dst[:, 40:64], src[:, 40:64])
+            wa_codes = keep([P, HALF], U32, "wa_codes%d" % h)
+            wa_plane = keep([P, HALF], U8, "wa_plane%d" % h)
+            nc.vector.quantize_mx(out=wa_codes[:].bitcast(FP8X4), scales=wa_plane[:], in_=wa_bf[:].rearrange("p n j -> p (n j)"))
+            for t in range(PACK):
+                bank = psum.tile([P, 512], F32, name="bank")
+                nc.tensor.matmul_mx(
+                    out=bank[:, 0:HALF],
+                    lhsT=x_codes[:, t * P : (t + 1) * P].bitcast(FP8X4),
+                    lhsT_scale=x_plane[:, t * P : (t + 1) * P],
+                    rhs=wa_codes[:].bitcast(FP8X4),
+                    rhs_scale=wa_plane[:],
+                    start=True,
+                    stop=True,
+                )
+                nc.scalar.copy(y[t][:, h * HALF : (h + 1) * HALF], bank[:, 0:HALF])
+
+        gt_sign = keep([P, PACK], F32, "gt_sign")
+        nc.scalar.activation(gt_sign[:], gt_sb[:], ACT.Sign)
+        w1_bf = keep([P, PACK, N], BF16, "w1_bf")
+        for j in range(PACK):
+            nc.scalar.activation(
+                w1_bf[:, j, :].rearrange("p (t m) -> p m t", t=PACK),
+                w1_raw[j // 2][:, j % 2, :].rearrange("p (m t) -> p m t", t=PACK),
+                ACT.Copy,
+                scale=gt_sign[:, j : j + 1],
+            )
+        w1_codes = [keep([P, P], U32, "w1_codes%d" % t) for t in range(PACK)]
+        w1_plane = [keep([P, P], U8, "w1_plane%d" % t) for t in range(PACK)]
+        hid = [keep([P, H], F32, "hid%d" % t) for t in range(PACK)]
+        sig0 = keep([P, H], F32, "sig0")
+        z_codes = [keep([P, HALF], U32, "z_codes%d" % c) for c in range(2)]
+        z_plane = [keep([P, HALF], U8, "z_plane%d" % c) for c in range(2)]
+
+        def look_up(c, part_tags, planes_tag, order):
+            c0, c1 = c * HALF, (c + 1) * HALF
+            z_planes = keep([P, PACK, HALF], BF16, "z_planes%d" % c, planes_tag)
+            part = {}
+            for kind, t in order:
+                if kind == "tab":
+                    part[t] = keep([P, HALF], F32, "part%d_%d" % (c, t), part_tags[t])
+                    nc.vector.tensor_tensor(part[t][:], tab_sb[t][:].indirect(entries(n1_sb, c0, c1)), y[t][:, c0:c1], ALU.subtract)
+                else:
+                    diff = keep([P, HALF], F32, "diff%d_%d" % (c, t))
+                    nc.vector.tensor_tensor(diff[:], y[t][:].indirect(entries(n2_sb, c0, c1)), part[t][:], ALU.add)
+                    nc.scalar.activation(z_planes[:, t, :], diff[:], ACT.Abs, scale=gt_sb[:, t : t + 1])
+            return z_planes
+
+        def quantise(codes, plane, woven):
+            nc.vector.quantize_mx(out=codes.bitcast(FP8X4), scales=plane, in_=woven.rearrange("p n t -> p (n t)"))
+
+        def second_product(c, t):
+            bank = psum.tile([P, 512], F32, name="bank")
+            nc.tensor.matmul_mx(
+                out=bank[:, 0:HALF],
+                lhsT=w1_codes[t][:].bitcast(FP8X4),
+                lhsT_scale=w1_plane[t][:],
+                rhs=z_codes[c][:].bitcast(FP8X4),
+                rhs_scale=z_plane[c][:],
+                start=True,
+                stop=True,
+            )
+            if t == 0:
+                nc.scalar.activation(sig0[:, c * HALF : (c + 1) * HALF], bank[:, 0:HALF], ACT.Sigmoid)
+            nc.scalar.copy(hid[t][:, c * HALF : (c + 1) * HALF], bank[:, 0:HALF])
+
+        def w1_columns(t):
+            return w1_bf[:, :, t * P : (t + 1) * P].rearrange("p j m -> p m j")
+
+        order0 = [("tab", 0), ("tab", 1), ("tab", 2), ("y", 0), ("tab", 3), ("y", 1), ("y", 2), ("y", 3)]
+        z_planes = look_up(0, ["part_a", "part_b", "part_c", "part_d"], "w1_raw1", order0)
+        z_woven = keep([P, HALF, PACK], BF16, "z_woven0")
+        nc.scalar.copy(z_woven[:], z_planes[:].rearrange("p t n -> p n t"))
+        w1_woven = keep([P, P, PACK], BF16, "w1_woven0")
+        nc.scalar.copy(w1_woven[:], w1_columns(0))
+        quantise(z_codes[0][:], z_plane[0][:], z_woven[:])
+        quantise(w1_codes[0][:], w1_plane[0][:], w1_woven[:])
+        second_product(0, 0)
+
+        order1 = [("tab", 0), ("tab", 1), ("y", 0), ("tab", 2), ("y", 1), ("tab", 3), ("y", 2), ("y", 3)]
+        z_planes = look_up(1, ["part_c", "part_d", "z_woven0", "w1_woven0"], None, order1)
+        z_woven = keep([P, HALF, PACK], BF16, "z_woven1")
+        nc.vector.tensor_copy(z_woven[:], z_planes[:].rearrange("p t n -> p n t"))
+        quantise(z_codes[1][:], z_plane[1][:], z_woven[:])
+        second_product(1, 0)
+
+        w1_rest = keep([P, 3 * P, PACK], BF16, "w1_rest", "w1_woven0")
+
+        def rest_products(t):
+            woven = w1_rest[:, (t - 1) * P : t * P, :]
+            nc.vector.tensor_copy(woven, w1_columns(t))
+            quantise(w1_codes[t][:], w1_plane[t][:], woven)
+            for c in range(2):
+                second_product(c, t)
+
+        out_rows = out.rearrange("(p t) n -> p t n", t=PACK)
+        st = [keep([P, H], F32, "st%d" % t) for t in range(PACK)]
+        other = [keep([P, H], F32, "other%d" % t) for t in range(PACK)]
+
+        def gate(t, h):
+            c0, c1 = h * HALF, (h + 1) * HALF
+            if t == 0:
+                nc.vector.tensor_tensor(st[t][:, c0:c1], sig0[:].indirect(entries(n3_sb, c0, c1)), hid[t][:, c0:c1], ALU.mult)
+            else:
+                sig = keep([P, HALF], F32, "sig%d_%d" % (t, h))
+                nc.scalar.activation(sig[:], hid[t][:].indirect(entries(n3_sb, c0, c1)), ACT.Sigmoid)
+                nc.vector.tensor_tensor(st[t][:, c0:c1], hid[t][:, c0:c1], sig[:], ALU.mult)
+
+        def fetch(t, h):
+            c0, c1 = h * HALF, (h + 1) * HALF
+            nc.vector.tensor_copy(other[t][:, c0:c1], st[t][:].indirect(entries(n3_sb, c0, c1)))
+
+        def larger(t, h):
+            c0, c1 = h * HALF, (h + 1) * HALF
+            res = keep([P, HALF], F32, "res%d_%d" % (t, h))
+            nc.vector.tensor_tensor(res[:], st[t][:, c0:c1], other[t][:, c0:c1], ALU.max)
+            nc.sync.dma_start(out_rows[:, t, c0:c1], res[:])
+
+        rest_products(1)
+        gate(0, 0)
+        gate(0, 1)
+        rest_products(2)
+        rest_products(3)
+        for t in range(PACK):
+            if t + 1 < PACK:
+                gate(t + 1, 0)
+            fetch(t, 0)
+            fetch(t, 1)
+            if t + 1 < PACK:
+                gate(t + 1, 1)
+            larger(t, 0)
+            larger(t, 1)

@@ -25,10 +25,10 @@ def tile_picked_tokkinddtwicp_none_p_kernel(tc, x_words, x_scales, wa, tab, gt, 
     nc = tc.nc
     with ExitStack() as ctx:
         held = ctx.enter_context(tc.tile_pool(name="held", bufs=1))
-        psum = ctx.enter_context(tc.psum_pool(name="psum", bufs=8))
+        psum = ctx.enter_context(tc.psum_pool(name="psum", bufs=1))
 
-        def keep(shape, dtype, name, tag=None):
-            return held.tile(shape, dtype, name=name, tag=tag or name, align_bytes=64)
+        def keep(shape, dtype, name):
+            return held.tile(shape, dtype, name=name, align_bytes=64)
 
         def entries(lst, c0, c1):
             return lst[:, c0 // 16 : c1 // 16]
@@ -43,55 +43,54 @@ def tile_picked_tokkinddtwicp_none_p_kernel(tc, x_words, x_scales, wa, tab, gt, 
 
         warm = keep([P, 8], F32, "warm")
         nc.gpsimd.memset(warm[:], 0.0)
-        warm2 = keep([P, 8], F32, "warm2")
-        nc.scalar.activation(warm2[:], warm[:], ACT.Sigmoid)
+        sig0 = keep([P, H], F32, "sig0")
+        nc.scalar.activation(sig0[:, 0:8], warm[:], ACT.Sigmoid)
 
-        words_hbm = x_words[0].rearrange("p n t -> p (n t)").bitcast(I32)
-        nc.sync.dma_start(offs_sb[:], offs)
-        nc.sync.dma_start(words_all[:, 0 : T // 2], words_hbm[:, 0 : T // 2])
-        for q in range(4):
-            nc.sync.dma_start(scales_all[32 * q : 32 * q + 4, :].bitcast(I32), x_scales[0, 4 * q : 4 * q + 4, :].bitcast(I32))
-        nc.sync.dma_start(words_all[:, T // 2 : T], words_hbm[:, T // 2 : T])
         wa_rows = wa.rearrange("(p j) n -> p j n", j=PACK)
         wa_raw = [keep([P, PACK, HALF], F32, "wa_raw%d" % h) for h in range(2)]
-        for h in range(2):
-            nc.sync.dma_start(wa_raw[h][:], wa_rows[:, :, h * HALF : (h + 1) * HALF])
-        nc.sync.dma_start(n1_sb[:], n1)
         tab_rows = tab.rearrange("(p t) n -> p t n", t=PACK)
         tab_sb = [keep([P, H], F32, "tab%d" % t) for t in range(PACK)]
-        for t in range(PACK):
-            nc.sync.dma_start(tab_sb[t][:], tab_rows[:, t, :])
-        nc.sync.dma_start(n2_sb[:], n2)
         gt_sb = keep([P, PACK], F32, "gt_sb")
+        w1_rows = w1.rearrange("(p j) n -> p (j n)", j=PACK)
+        w1_raw = [keep([P, 2 * N], F32, "w1_raw%d" % u) for u in range(2)]
+        nc.sync.dma_start(offs_sb[:], offs)
+        words_hbm = x_words[0].rearrange("p n t -> p (n t)").bitcast(I32)
+        nc.sync.dma_start(words_all[:, 0 : T // 4], words_hbm[:, 0 : T // 4])
+        for q in range(4):
+            nc.sync.dma_start(scales_all[32 * q : 32 * q + 4, :].bitcast(I32), x_scales[0, 4 * q : 4 * q + 4, :].bitcast(I32))
+        nc.sync.dma_start(words_all[:, T // 4 : T], words_hbm[:, T // 4 : T])
+        nc.sync.dma_start(wa_raw[0][:], wa_rows[:, :, 0:HALF])
+        nc.sync.dma_start(wa_raw[1][:], wa_rows[:, :, HALF:H])
+        nc.sync.dma_start(n1_sb[:], n1)
+        nc.sync.dma_start(tab_sb[0][:], tab_rows[:, 0, :])
+        nc.sync.dma_start(tab_sb[1][:], tab_rows[:, 1, :])
+        nc.sync.dma_start(n2_sb[:], n2)
         nc.sync.dma_start(gt_sb[:], gt.rearrange("(p t) o -> p (t o)", t=PACK))
-        w1_rows = w1.rearrange("(p j) n -> p j n", j=PACK)
-        w1_raw = [keep([P, 2, N], F32, "w1_raw%d" % u) for u in range(2)]
-        for u in range(2):
-            nc.sync.dma_start(w1_raw[u][:], w1_rows[:, 2 * u : 2 * u + 2, :])
+        nc.sync.dma_start(tab_sb[2][:], tab_rows[:, 2, :])
+        nc.sync.dma_start(tab_sb[3][:], tab_rows[:, 3, :])
+        nc.sync.dma_start(w1_raw[0][:], w1_rows[:, 0 : 2 * N])
+        nc.sync.dma_start(w1_raw[1][:], w1_rows[:, 2 * N : 4 * N])
         nc.sync.dma_start(n3_sb[:], n3)
 
         scales_got = keep([P, S], U8, "scales_got")
         nc.vector.tensor_copy(scales_got[:], scales_all[:].indirect(offs_sb[:]))
-        x_codes = keep([P, S], U32, "x_codes")
-        nc.vector.tensor_copy(x_codes[:].rearrange("p (t m) -> p m t", t=PACK), words_all[:].bitcast(U32).indirect(offs_sb[:]))
         x_plane = keep([P, S], U8, "x_plane")
         nc.vector.tensor_copy(x_plane[:].rearrange("p (t m) -> p t m", t=PACK), scales_got[:].rearrange("p (m t) -> p t m", t=PACK))
+        x_codes = keep([P, S], U32, "x_codes")
+        nc.vector.tensor_copy(x_codes[:].rearrange("p (t m) -> p m t", t=PACK), words_all[:].bitcast(U32).indirect(offs_sb[:]))
 
         y = [keep([P, H], F32, "y%d" % t) for t in range(PACK)]
         for h in range(2):
             wa_bf = keep([P, HALF, PACK], BF16, "wa_bf%d" % h)
             dst = wa_bf[:].rearrange("p (c i) j -> p c j i", i=4)
             src = wa_raw[h][:].rearrange("p j (c i) -> p c j i", i=4)
-            if h == 0:
-                nc.scalar.copy(dst, src)
-            else:
-                nc.vector.tensor_copy(dst[:, 0:40], src[:, 0:40])
-                nc.scalar.copy(dst[:, 40:64], src[:, 40:64])
+            nc.vector.tensor_copy(dst[:, 0:40], src[:, 0:40])
+            nc.scalar.copy(dst[:, 40:64], src[:, 40:64])
             wa_codes = keep([P, HALF], U32, "wa_codes%d" % h)
             wa_plane = keep([P, HALF], U8, "wa_plane%d" % h)
             nc.vector.quantize_mx(out=wa_codes[:].bitcast(FP8X4), scales=wa_plane[:], in_=wa_bf[:].rearrange("p n j -> p (n j)"))
             for t in range(PACK):
-                bank = psum.tile([P, 512], F32, name="bank")
+                bank = psum.tile([P, 512], F32, name="bank%d" % (PACK * h + t))
                 nc.tensor.matmul_mx(
                     out=bank[:, 0:HALF],
                     lhsT=x_codes[:, t * P : (t + 1) * P].bitcast(FP8X4),
@@ -109,112 +108,113 @@ def tile_picked_tokkinddtwicp_none_p_kernel(tc, x_words, x_scales, wa, tab, gt, 
         for j in range(PACK):
             nc.scalar.activation(
                 w1_bf[:, j, :].rearrange("p (t m) -> p m t", t=PACK),
-                w1_raw[j // 2][:, j % 2, :].rearrange("p (m t) -> p m t", t=PACK),
+                w1_raw[j // 2][:, (j % 2) * N : (j % 2 + 1) * N].rearrange("p (m t) -> p m t", t=PACK),
                 ACT.Copy,
                 scale=gt_sign[:, j : j + 1],
             )
         w1_codes = [keep([P, P], U32, "w1_codes%d" % t) for t in range(PACK)]
         w1_plane = [keep([P, P], U8, "w1_plane%d" % t) for t in range(PACK)]
-        hid = [keep([P, H], F32, "hid%d" % t) for t in range(PACK)]
-        sig0 = keep([P, H], F32, "sig0")
-        z_codes = [keep([P, HALF], U32, "z_codes%d" % c) for c in range(2)]
-        z_plane = [keep([P, HALF], U8, "z_plane%d" % c) for c in range(2)]
+        wide = [keep([P, 2 * H], F32, "wide%d" % t) for t in range(PACK)]
+        hid = [wide[0][:, H : 2 * H]] + [keep([P, H], F32, "hid%d" % t)[:] for t in range(1, PACK)]
+        z_codes = keep([P, H], U32, "z_codes")
+        z_plane = keep([P, H], U8, "z_plane")
 
-        def look_up(c, part_tags, planes_tag, order):
+        z_planes = w1_raw[1][:, N : 2 * N].bitcast(BF16).rearrange("p (t n) -> p t n", t=PACK)
+
+        def look_up(c, part, order):
             c0, c1 = c * HALF, (c + 1) * HALF
-            z_planes = keep([P, PACK, HALF], BF16, "z_planes%d" % c, planes_tag)
-            part = {}
             for kind, t in order:
                 if kind == "tab":
-                    part[t] = keep([P, HALF], F32, "part%d_%d" % (c, t), part_tags[t])
-                    nc.vector.tensor_tensor(part[t][:], tab_sb[t][:].indirect(entries(n1_sb, c0, c1)), y[t][:, c0:c1], ALU.subtract)
+                    nc.vector.tensor_tensor(part[t], tab_sb[t][:].indirect(entries(n1_sb, c0, c1)), y[t][:, c0:c1], ALU.subtract)
                 else:
                     diff = keep([P, HALF], F32, "diff%d_%d" % (c, t))
-                    nc.vector.tensor_tensor(diff[:], y[t][:].indirect(entries(n2_sb, c0, c1)), part[t][:], ALU.add)
+                    nc.vector.tensor_tensor(diff[:], y[t][:].indirect(entries(n2_sb, c0, c1)), part[t], ALU.add)
                     nc.scalar.activation(z_planes[:, t, :], diff[:], ACT.Abs, scale=gt_sb[:, t : t + 1])
-            return z_planes
 
         def quantise(codes, plane, woven):
-            nc.vector.quantize_mx(out=codes.bitcast(FP8X4), scales=plane, in_=woven.rearrange("p n t -> p (n t)"))
+            nc.vector.quantize_mx(out=codes.bitcast(FP8X4), scales=plane, in_=woven)
 
-        def second_product(c, t):
-            bank = psum.tile([P, 512], F32, name="bank")
+        def second_product(t, c0, c1, bank_name):
+            bank = psum.tile([P, 512], F32, name=bank_name)
             nc.tensor.matmul_mx(
-                out=bank[:, 0:HALF],
+                out=bank[:, 0 : c1 - c0],
                 lhsT=w1_codes[t][:].bitcast(FP8X4),
                 lhsT_scale=w1_plane[t][:],
-                rhs=z_codes[c][:].bitcast(FP8X4),
-                rhs_scale=z_plane[c][:],
+                rhs=z_codes[:, c0:c1].bitcast(FP8X4),
+                rhs_scale=z_plane[:, c0:c1],
                 start=True,
                 stop=True,
             )
             if t == 0:
-                nc.scalar.activation(sig0[:, c * HALF : (c + 1) * HALF], bank[:, 0:HALF], ACT.Sigmoid)
-            nc.scalar.copy(hid[t][:, c * HALF : (c + 1) * HALF], bank[:, 0:HALF])
+                nc.scalar.activation(sig0[:, c0:c1], bank[:, 0 : c1 - c0], ACT.Sigmoid)
+            nc.scalar.copy(hid[t][:, c0:c1], bank[:, 0 : c1 - c0])
+
+        def by_word(woven):
+            return woven.rearrange("p (n t) -> p n t", t=PACK)
 
         def w1_columns(t):
             return w1_bf[:, :, t * P : (t + 1) * P].rearrange("p j m -> p m j")
 
-        order0 = [("tab", 0), ("tab", 1), ("tab", 2), ("y", 0), ("tab", 3), ("y", 1), ("y", 2), ("y", 3)]
-        z_planes = look_up(0, ["part_a", "part_b", "part_c", "part_d"], "w1_raw1", order0)
-        z_woven = keep([P, HALF, PACK], BF16, "z_woven0")
-        nc.scalar.copy(z_woven[:], z_planes[:].rearrange("p t n -> p n t"))
-        w1_woven = keep([P, P, PACK], BF16, "w1_woven0")
-        nc.scalar.copy(w1_woven[:], w1_columns(0))
-        quantise(z_codes[0][:], z_plane[0][:], z_woven[:])
-        quantise(w1_codes[0][:], w1_plane[0][:], w1_woven[:])
-        second_product(0, 0)
+        order0 = [("tab", 0), ("tab", 1), ("y", 0), ("tab", 2), ("y", 1), ("tab", 3), ("y", 2), ("y", 3)]
+        part = [keep([P, HALF], F32, "part%d" % t)[:] for t in range(PACK)]
+        look_up(0, part, order0)
+        z_woven = keep([P, HALF * PACK], BF16, "z_woven0")
+        w1_woven = [keep([P, P * PACK], BF16, "w1_woven%d" % t) for t in range(PACK)]
+        nc.scalar.copy(by_word(w1_woven[0][:]), w1_columns(0))
+        nc.scalar.copy(by_word(z_woven[:]), z_planes.rearrange("p t n -> p n t"))
+        for t in range(1, PACK):
+            nc.scalar.copy(by_word(w1_woven[t][:]), w1_columns(t))
+        quantise(w1_codes[0][:], w1_plane[0][:], w1_woven[0][:])
+        quantise(z_codes[:, 0:HALF], z_plane[:, 0:HALF], z_woven[:])
+        second_product(0, 0, HALF, "bank0")
 
-        order1 = [("tab", 0), ("tab", 1), ("y", 0), ("tab", 2), ("y", 1), ("tab", 3), ("y", 2), ("y", 3)]
-        z_planes = look_up(1, ["part_c", "part_d", "z_woven0", "w1_woven0"], None, order1)
-        z_woven = keep([P, HALF, PACK], BF16, "z_woven1")
-        nc.vector.tensor_copy(z_woven[:], z_planes[:].rearrange("p t n -> p n t"))
-        quantise(z_codes[1][:], z_plane[1][:], z_woven[:])
-        second_product(1, 0)
-
-        w1_rest = keep([P, 3 * P, PACK], BF16, "w1_rest", "w1_woven0")
+        order1 = [("tab", 0), ("tab", 1), ("y", 0), ("y", 1), ("tab", 2), ("tab", 3), ("y", 2), ("y", 3)]
+        look_up(1, [part[2], part[3], z_woven[:].bitcast(F32)[:, 0:HALF], z_woven[:].bitcast(F32)[:, HALF:H]], order1)
+        z_woven = keep([P, HALF * PACK], BF16, "z_woven1")
+        nc.vector.tensor_copy(by_word(z_woven[:])[:, 0:160, :], z_planes[:, :, 0:160].rearrange("p t n -> p n t"))
+        nc.scalar.copy(by_word(z_woven[:])[:, 160:HALF, :], z_planes[:, :, 160:HALF].rearrange("p t n -> p n t"))
+        quantise(z_codes[:, HALF:H], z_plane[:, HALF:H], z_woven[:])
+        second_product(0, HALF, H, "bank4")
 
         def rest_products(t):
-            woven = w1_rest[:, (t - 1) * P : t * P, :]
-            nc.vector.tensor_copy(woven, w1_columns(t))
-            quantise(w1_codes[t][:], w1_plane[t][:], woven)
-            for c in range(2):
-                second_product(c, t)
+            quantise(w1_codes[t][:], w1_plane[t][:], w1_woven[t][:])
+            second_product(t, 0, H, "bank%d" % t)
 
         out_rows = out.rearrange("(p t) n -> p t n", t=PACK)
-        st = [keep([P, H], F32, "st%d" % t) for t in range(PACK)]
         other = [keep([P, H], F32, "other%d" % t) for t in range(PACK)]
+        halves = [(0, HALF), (HALF, H)]
 
-        def gate(t, h):
-            c0, c1 = h * HALF, (h + 1) * HALF
+        def gate(t):
             if t == 0:
-                nc.vector.tensor_tensor(st[t][:, c0:c1], sig0[:].indirect(entries(n3_sb, c0, c1)), hid[t][:, c0:c1], ALU.mult)
+                for c0, c1 in halves:
+                    nc.vector.tensor_tensor(wide[t][:, c0:c1], sig0[:].indirect(entries(n3_sb, c0, c1)), hid[t][:, c0:c1], ALU.mult)
             else:
-                sig = keep([P, HALF], F32, "sig%d_%d" % (t, h))
-                nc.scalar.activation(sig[:], hid[t][:].indirect(entries(n3_sb, c0, c1)), ACT.Sigmoid)
-                nc.vector.tensor_tensor(st[t][:, c0:c1], hid[t][:, c0:c1], sig[:], ALU.mult)
+                for c0, c1 in halves:
+                    nc.scalar.activation(wide[t][:, H + c0 : H + c1], hid[t].indirect(entries(n3_sb, c0, c1)), ACT.Sigmoid)
+                nc.vector.tensor_tensor(wide[t][:, 0:H], hid[t], wide[t][:, H : 2 * H], ALU.mult)
 
-        def fetch(t, h):
-            c0, c1 = h * HALF, (h + 1) * HALF
-            nc.vector.tensor_copy(other[t][:, c0:c1], st[t][:].indirect(entries(n3_sb, c0, c1)))
+        def fetch(t, c0, c1):
+            nc.vector.tensor_copy(other[t][:, c0:c1], wide[t][:].indirect(entries(n3_sb, c0, c1)))
 
-        def larger(t, h):
-            c0, c1 = h * HALF, (h + 1) * HALF
-            res = keep([P, HALF], F32, "res%d_%d" % (t, h))
-            nc.vector.tensor_tensor(res[:], st[t][:, c0:c1], other[t][:, c0:c1], ALU.max)
+        def larger(t, c0, c1):
+            res = keep([P, c1 - c0], F32, "res%d_%d" % (t, c0))
+            nc.vector.tensor_tensor(res[:], wide[t][:, c0:c1], other[t][:, c0:c1], ALU.max)
             nc.sync.dma_start(out_rows[:, t, c0:c1], res[:])
 
         rest_products(1)
-        gate(0, 0)
-        gate(0, 1)
+        gate(0)
         rest_products(2)
         rest_products(3)
-        for t in range(PACK):
-            if t + 1 < PACK:
-                gate(t + 1, 0)
-            fetch(t, 0)
-            fetch(t, 1)
-            if t + 1 < PACK:
-                gate(t + 1, 1)
-            larger(t, 0)
-            larger(t, 1)
+        gate(1)
+        fetch(0, 0, H)
+        gate(2)
+        larger(0, 0, H)
+        fetch(1, 0, H)
+        gate(3)
+        larger(1, 0, H)
+        fetch(2, 0, H)
+        fetch(3, 0, HALF)
+        larger(2, 0, H)
+        fetch(3, HALF, H)
+        larger(3, 0, HALF)
+        larger(3, HALF, H)

@@ -49,7 +49,9 @@ def tile_picked_tokkinddtwicp_none_p_kernel(tc, x_words, x_scales, wa, tab, gt, 
         wa_rows = wa.rearrange("(p j) n -> p j n", j=PACK)
         wa_raw = [keep([P, PACK, HALF], F32, "wa_raw%d" % h) for h in range(2)]
         tab_rows = tab.rearrange("(p t) n -> p t n", t=PACK)
-        tab_sb = [keep([P, H], F32, "tab%d" % t) for t in range(PACK)]
+        tab_sb = [keep([P, H if t < 2 else 2 * H], F32, "tab%d" % t) for t in range(PACK)]
+        for t in range(2, PACK):
+            nc.gpsimd.memset(tab_sb[t][:, H : 2 * H], 0.0)
         gt_sb = keep([P, PACK], F32, "gt_sb")
         w1_rows = w1.rearrange("(p j) n -> p (j n)", j=PACK)
         w1_raw = [keep([P, 2 * N], F32, "w1_raw%d" % u) for u in range(2)]
@@ -66,8 +68,8 @@ def tile_picked_tokkinddtwicp_none_p_kernel(tc, x_words, x_scales, wa, tab, gt, 
         nc.sync.dma_start(tab_sb[1][:], tab_rows[:, 1, :])
         nc.sync.dma_start(n2_sb[:], n2)
         nc.sync.dma_start(gt_sb[:], gt.rearrange("(p t) o -> p (t o)", t=PACK))
-        nc.sync.dma_start(tab_sb[2][:], tab_rows[:, 2, :])
-        nc.sync.dma_start(tab_sb[3][:], tab_rows[:, 3, :])
+        nc.sync.dma_start(tab_sb[2][:, 0:H], tab_rows[:, 2, :])
+        nc.sync.dma_start(tab_sb[3][:, 0:H], tab_rows[:, 3, :])
         nc.sync.dma_start(w1_raw[0][:], w1_rows[:, 0 : 2 * N])
         nc.sync.dma_start(w1_raw[1][:], w1_rows[:, 2 * N : 4 * N])
         nc.sync.dma_start(n3_sb[:], n3)
@@ -114,22 +116,19 @@ def tile_picked_tokkinddtwicp_none_p_kernel(tc, x_words, x_scales, wa, tab, gt, 
             )
         w1_codes = [keep([P, P], U32, "w1_codes%d" % t) for t in range(PACK)]
         w1_plane = [keep([P, P], U8, "w1_plane%d" % t) for t in range(PACK)]
-        wide = [keep([P, 2 * H], F32, "wide%d" % t) for t in range(PACK)]
+        wide = [keep([P, 2 * H], F32, "wide%d" % t) for t in range(2)] * 2
         hid = [wide[0][:, H : 2 * H]] + [keep([P, H], F32, "hid%d" % t)[:] for t in range(1, PACK)]
         z_codes = keep([P, H], U32, "z_codes")
         z_plane = keep([P, H], U8, "z_plane")
 
         z_planes = w1_raw[1][:, N : 2 * N].bitcast(BF16).rearrange("p (t n) -> p t n", t=PACK)
 
-        def look_up(c, part, order):
-            c0, c1 = c * HALF, (c + 1) * HALF
-            for kind, t in order:
-                if kind == "tab":
-                    nc.vector.tensor_tensor(part[t], tab_sb[t][:].indirect(entries(n1_sb, c0, c1)), y[t][:, c0:c1], ALU.subtract)
-                else:
-                    diff = keep([P, HALF], F32, "diff%d_%d" % (c, t))
-                    nc.vector.tensor_tensor(diff[:], y[t][:].indirect(entries(n2_sb, c0, c1)), part[t], ALU.add)
-                    nc.scalar.activation(z_planes[:, t, :], diff[:], ACT.Abs, scale=gt_sb[:, t : t + 1])
+        def less_y(t, c0, c1, part):
+            nc.vector.tensor_tensor(part, tab_sb[t][:].indirect(entries(n1_sb, c0, c1)), y[t][:, c0:c1], ALU.subtract)
+
+        def size(t, c0, c1, part, diff):
+            nc.vector.tensor_tensor(diff, y[t][:].indirect(entries(n2_sb, c0, c1)), part, ALU.add)
+            nc.scalar.activation(z_planes[:, t, :], diff, ACT.Abs, scale=gt_sb[:, t : t + 1])
 
         def quantise(codes, plane, woven):
             nc.vector.quantize_mx(out=codes.bitcast(FP8X4), scales=plane, in_=woven)
@@ -145,9 +144,12 @@ def tile_picked_tokkinddtwicp_none_p_kernel(tc, x_words, x_scales, wa, tab, gt, 
                 start=True,
                 stop=True,
             )
-            if t == 0:
-                nc.scalar.activation(sig0[:, c0:c1], bank[:, 0 : c1 - c0], ACT.Sigmoid)
-            nc.scalar.copy(hid[t][:, c0:c1], bank[:, 0 : c1 - c0])
+            return bank[:, 0 : c1 - c0]
+
+        def first_tile(c0, c1, bank_name):
+            bank = second_product(0, c0, c1, bank_name)
+            nc.scalar.activation(sig0[:, c0:c1], bank, ACT.Sigmoid)
+            nc.scalar.copy(hid[0][:, c0:c1], bank)
 
         def by_word(woven):
             return woven.rearrange("p (n t) -> p n t", t=PACK)
@@ -155,9 +157,16 @@ def tile_picked_tokkinddtwicp_none_p_kernel(tc, x_words, x_scales, wa, tab, gt, 
         def w1_columns(t):
             return w1_bf[:, :, t * P : (t + 1) * P].rearrange("p j m -> p m j")
 
-        order0 = [("tab", 0), ("tab", 1), ("y", 0), ("tab", 2), ("y", 1), ("tab", 3), ("y", 2), ("y", 3)]
-        part = [keep([P, HALF], F32, "part%d" % t)[:] for t in range(PACK)]
-        look_up(0, part, order0)
+        part = [keep([P, HALF if t < 2 else H], F32, "part%d" % t) for t in range(PACK)]
+        diff = [keep([P, HALF], F32, "diff%d" % i) for i in range(PACK + 2)]
+        less_y(0, 0, HALF, part[0][:])
+        less_y(1, 0, HALF, part[1][:])
+        size(0, 0, HALF, part[0][:], diff[0][:])
+        less_y(2, 0, H, part[2][:])
+        size(1, 0, HALF, part[1][:], diff[1][:])
+        less_y(3, 0, H, part[3][:])
+        size(2, 0, HALF, part[2][:, 0:HALF], diff[2][:])
+        size(3, 0, HALF, part[3][:, 0:HALF], diff[3][:])
         z_woven = keep([P, HALF * PACK], BF16, "z_woven0")
         w1_woven = [keep([P, P * PACK], BF16, "w1_woven%d" % t) for t in range(PACK)]
         nc.scalar.copy(by_word(w1_woven[0][:]), w1_columns(0))
@@ -166,19 +175,25 @@ def tile_picked_tokkinddtwicp_none_p_kernel(tc, x_words, x_scales, wa, tab, gt, 
             nc.scalar.copy(by_word(w1_woven[t][:]), w1_columns(t))
         quantise(w1_codes[0][:], w1_plane[0][:], w1_woven[0][:])
         quantise(z_codes[:, 0:HALF], z_plane[:, 0:HALF], z_woven[:])
-        second_product(0, 0, HALF, "bank0")
+        first_tile(0, HALF, "bank0")
 
-        order1 = [("tab", 0), ("tab", 1), ("y", 0), ("y", 1), ("tab", 2), ("tab", 3), ("y", 2), ("y", 3)]
-        look_up(1, [part[2], part[3], z_woven[:].bitcast(F32)[:, 0:HALF], z_woven[:].bitcast(F32)[:, HALF:H]], order1)
+        less_y(0, HALF, H, part[2][:, 0:HALF])
+        less_y(1, HALF, H, part[3][:, 0:HALF])
+        size(0, HALF, H, part[2][:, 0:HALF], diff[4][:])
+        size(1, HALF, H, part[3][:, 0:HALF], diff[5][:])
+        spent = z_woven[:].bitcast(F32)
+        size(2, HALF, H, part[2][:, HALF:H], spent[:, 0:HALF])
+        size(3, HALF, H, part[3][:, HALF:H], spent[:, HALF:H])
         z_woven = keep([P, HALF * PACK], BF16, "z_woven1")
         nc.vector.tensor_copy(by_word(z_woven[:])[:, 0:160, :], z_planes[:, :, 0:160].rearrange("p t n -> p n t"))
         nc.scalar.copy(by_word(z_woven[:])[:, 160:HALF, :], z_planes[:, :, 160:HALF].rearrange("p t n -> p n t"))
         quantise(z_codes[:, HALF:H], z_plane[:, HALF:H], z_woven[:])
-        second_product(0, HALF, H, "bank4")
+        first_tile(HALF, H, "bank4")
 
-        def rest_products(t):
+        banks = {}
+        for t in range(1, PACK):
             quantise(w1_codes[t][:], w1_plane[t][:], w1_woven[t][:])
-            second_product(t, 0, H, "bank%d" % t)
+            banks[t] = second_product(t, 0, H, "bank%d" % t)
 
         out_rows = out.rearrange("(p t) n -> p t n", t=PACK)
         other = [keep([P, H], F32, "other%d" % t) for t in range(PACK)]
@@ -189,9 +204,12 @@ def tile_picked_tokkinddtwicp_none_p_kernel(tc, x_words, x_scales, wa, tab, gt, 
                 for c0, c1 in halves:
                     nc.vector.tensor_tensor(wide[t][:, c0:c1], sig0[:].indirect(entries(n3_sb, c0, c1)), hid[t][:, c0:c1], ALU.mult)
             else:
+                nc.scalar.copy(hid[t], banks[t])
+                sig = wide[1][:, H : 2 * H] if t == 1 else keep([P, H], F32, "sig%d" % t)[:]
                 for c0, c1 in halves:
-                    nc.scalar.activation(wide[t][:, H + c0 : H + c1], hid[t].indirect(entries(n3_sb, c0, c1)), ACT.Sigmoid)
-                nc.vector.tensor_tensor(wide[t][:, 0:H], hid[t], wide[t][:, H : 2 * H], ALU.mult)
+                    nc.scalar.activation(sig[:, c0:c1], hid[t].indirect(entries(n3_sb, c0, c1)), ACT.Sigmoid)
+                engine = nc.vector if t == 1 else nc.gpsimd
+                engine.tensor_tensor(wide[t][:, 0:H], hid[t], sig, ALU.mult)
 
         def fetch(t, c0, c1):
             nc.vector.tensor_copy(other[t][:, c0:c1], wide[t][:].indirect(entries(n3_sb, c0, c1)))
@@ -201,20 +219,17 @@ def tile_picked_tokkinddtwicp_none_p_kernel(tc, x_words, x_scales, wa, tab, gt, 
             nc.vector.tensor_tensor(res[:], wide[t][:, c0:c1], other[t][:, c0:c1], ALU.max)
             nc.sync.dma_start(out_rows[:, t, c0:c1], res[:])
 
-        rest_products(1)
         gate(0)
-        rest_products(2)
-        rest_products(3)
-        gate(1)
         fetch(0, 0, H)
-        gate(2)
+        gate(1)
         larger(0, 0, H)
         fetch(1, 0, H)
-        gate(3)
+        gate(2)
         larger(1, 0, H)
         fetch(2, 0, H)
-        fetch(3, 0, HALF)
+        gate(3)
         larger(2, 0, H)
+        fetch(3, 0, HALF)
         fetch(3, HALF, H)
         larger(3, 0, HALF)
         larger(3, HALF, H)

@@ -18,7 +18,7 @@ ACT = mybir.ActivationFunctionType
 P = 128
 PACK = 4
 HALF = 256
-CHUNKS = [(0, 256), (256, 512)]
+WA_ON_VECTOR = (26, 40)
 
 
 def tile_picked_tokkinddtwicp_none_p_kernel(tc, x_words, x_scales, wa, tab, gt, w1, offs, n1, n2, n3, out):
@@ -42,7 +42,7 @@ def tile_picked_tokkinddtwicp_none_p_kernel(tc, x_words, x_scales, wa, tab, gt, 
         nc.vector.memset(scales_all[:].bitcast(I32), 0)
 
         warm = keep([P, 8], F32, "warm")
-        nc.gpsimd.memset(warm[:], 0.0)
+        nc.vector.memset(warm[:], 0.0)
         sig0 = keep([P, H], F32, "sig0")
         nc.scalar.activation(sig0[:, 0:8], warm[:], ACT.Sigmoid)
 
@@ -51,7 +51,7 @@ def tile_picked_tokkinddtwicp_none_p_kernel(tc, x_words, x_scales, wa, tab, gt, 
         tab_rows = tab.rearrange("(p t) n -> p t n", t=PACK)
         tab_sb = [keep([P, H if t < 2 else 2 * H], F32, "tab%d" % t) for t in range(PACK)]
         for t in range(2, PACK):
-            nc.gpsimd.memset(tab_sb[t][:, H : 2 * H], 0.0)
+            nc.vector.memset(tab_sb[t][:, H : 2 * H], 0.0)
         gt_sb = keep([P, PACK], F32, "gt_sb")
         w1_rows = w1.rearrange("(p j) n -> p (j n)", j=PACK)
         w1_raw = [keep([P, 2 * N], F32, "w1_raw%d" % u) for u in range(2)]
@@ -86,8 +86,9 @@ def tile_picked_tokkinddtwicp_none_p_kernel(tc, x_words, x_scales, wa, tab, gt, 
             wa_bf = keep([P, HALF, PACK], BF16, "wa_bf%d" % h)
             dst = wa_bf[:].rearrange("p (c i) j -> p c j i", i=4)
             src = wa_raw[h][:].rearrange("p j (c i) -> p c j i", i=4)
-            nc.vector.tensor_copy(dst[:, 0:40], src[:, 0:40])
-            nc.scalar.copy(dst[:, 40:64], src[:, 40:64])
+            cut = WA_ON_VECTOR[h]
+            nc.vector.tensor_copy(dst[:, 0:cut], src[:, 0:cut])
+            nc.scalar.copy(dst[:, cut:64], src[:, cut:64])
             wa_codes = keep([P, HALF], U32, "wa_codes%d" % h)
             wa_plane = keep([P, HALF], U8, "wa_plane%d" % h)
             nc.vector.quantize_mx(out=wa_codes[:].bitcast(FP8X4), scales=wa_plane[:], in_=wa_bf[:].rearrange("p n j -> p (n j)"))
@@ -116,7 +117,7 @@ def tile_picked_tokkinddtwicp_none_p_kernel(tc, x_words, x_scales, wa, tab, gt, 
             )
         w1_codes = [keep([P, P], U32, "w1_codes%d" % t) for t in range(PACK)]
         w1_plane = [keep([P, P], U8, "w1_plane%d" % t) for t in range(PACK)]
-        wide = [keep([P, 2 * H], F32, "wide%d" % t) for t in range(2)] * 2
+        wide = [keep([P, 2 * H], F32, "wide%d" % t) for t in range(PACK)]
         hid = [wide[0][:, H : 2 * H]] + [keep([P, H], F32, "hid%d" % t)[:] for t in range(1, PACK)]
         z_codes = keep([P, H], U32, "z_codes")
         z_plane = keep([P, H], U8, "z_plane")
@@ -205,11 +206,10 @@ def tile_picked_tokkinddtwicp_none_p_kernel(tc, x_words, x_scales, wa, tab, gt, 
                     nc.vector.tensor_tensor(wide[t][:, c0:c1], sig0[:].indirect(entries(n3_sb, c0, c1)), hid[t][:, c0:c1], ALU.mult)
             else:
                 nc.scalar.copy(hid[t], banks[t])
-                sig = wide[1][:, H : 2 * H] if t == 1 else keep([P, H], F32, "sig%d" % t)[:]
+                sig = wide[t][:, H : 2 * H]
                 for c0, c1 in halves:
                     nc.scalar.activation(sig[:, c0:c1], hid[t].indirect(entries(n3_sb, c0, c1)), ACT.Sigmoid)
-                engine = nc.vector if t == 1 else nc.gpsimd
-                engine.tensor_tensor(wide[t][:, 0:H], hid[t], sig, ALU.mult)
+                nc.vector.tensor_tensor(wide[t][:, 0:H], hid[t], sig, ALU.mult)
 
         def fetch(t, c0, c1):
             nc.vector.tensor_copy(other[t][:, c0:c1], wide[t][:].indirect(entries(n3_sb, c0, c1)))

from contextlib import ExitStack

import concourse.mybir as mybir

K, T, S, N, H = 512, 2048, 512, 512, 512
FLOPS = 2 * K * S * H + 2 * S * N * H

F32 = mybir.dt.float32
BF16 = mybir.dt.bfloat16
I32 = mybir.dt.int32
U32 = mybir.dt.uint32
U16 = mybir.dt.uint16
U8 = mybir.dt.uint8
FP8X4 = mybir.dt.float8_e4m3fn_x4
ALU = mybir.AluOpType
ACT = mybir.ActivationFunctionType

P = 128
PACK = 4
HALF = 256
WA_ON_VECTOR = (26, 40)


def tile_picked_tokkinddtwicp_none_p_kernel(tc, x_words, x_scales, wa, tab, gt, w1, offs, n1, n2, n3, out):
    nc = tc.nc
    with ExitStack() as ctx:
        held = ctx.enter_context(tc.tile_pool(name="held", bufs=1))
        psum = ctx.enter_context(tc.psum_pool(name="psum", bufs=1))

        def keep(shape, dtype, name):
            return held.tile(shape, dtype, name=name, align_bytes=64)

        def entries(lst, c0, c1):
            return lst[:, c0 // 16 : c1 // 16]

        offs_sb = keep([P, 32], U16, "offs_sb")
        n1_sb = keep([P, 32], U16, "n1_sb")
        n2_sb = keep([P, 32], U16, "n2_sb")
        n3_sb = keep([P, 32], U16, "n3_sb")
        words_all = keep([P, T], I32, "words_all")
        scales_all = keep([P, T], U8, "scales_all")
        nc.vector.memset(scales_all[:].bitcast(I32), 0)

        warm = keep([P, 8], F32, "warm")
        nc.vector.memset(warm[:], 0.0)
        sig0 = keep([P, H], F32, "sig0")
        nc.scalar.activation(sig0[:, 0:8], warm[:], ACT.Sigmoid)

        wa_rows = wa.rearrange("(p j) n -> p j n", j=PACK)
        wa_raw = [keep([P, PACK, HALF], F32, "wa_raw%d" % h) for h in range(2)]
        tab_rows = tab.rearrange("(p t) n -> p t n", t=PACK)
        tab_sb = [keep([P, H if t < 2 else 2 * H], F32, "tab%d" % t) for t in range(PACK)]
        for t in range(2, PACK):
            nc.vector.memset(tab_sb[t][:, H : 2 * H], 0.0)
        gt_sb = keep([P, PACK], F32, "gt_sb")
        w1_rows = w1.rearrange("(p j) n -> p (j n)", j=PACK)
        w1_raw = [keep([P, 2 * N], F32, "w1_raw%d" % u) for u in range(2)]
        nc.sync.dma_start(offs_sb[:], offs)
        words_hbm = x_words[0].rearrange("p n t -> p (n t)").bitcast(I32)
        nc.sync.dma_start(words_all[:, 0 : T // 4], words_hbm[:, 0 : T // 4])
        for q in range(4):
            nc.sync.dma_start(scales_all[32 * q : 32 * q + 4, :].bitcast(I32), x_scales[0, 4 * q : 4 * q + 4, :].bitcast(I32))
        nc.sync.dma_start(words_all[:, T // 4 : T], words_hbm[:, T // 4 : T])
        nc.sync.dma_start(wa_raw[0][:], wa_rows[:, :, 0:HALF])
        nc.sync.dma_start(wa_raw[1][:], wa_rows[:, :, HALF:H])
        nc.sync.dma_start(n1_sb[:], n1)
        nc.sync.dma_start(tab_sb[0][:], tab_rows[:, 0, :])
        nc.sync.dma_start(tab_sb[1][:], tab_rows[:, 1, :])
        nc.sync.dma_start(n2_sb[:], n2)
        nc.sync.dma_start(gt_sb[:], gt.rearrange("(p t) o -> p (t o)", t=PACK))
        nc.sync.dma_start(tab_sb[2][:, 0:H], tab_rows[:, 2, :])
        nc.sync.dma_start(tab_sb[3][:, 0:H], tab_rows[:, 3, :])
        nc.sync.dma_start(w1_raw[0][:], w1_rows[:, 0 : 2 * N])
        nc.sync.dma_start(w1_raw[1][:], w1_rows[:, 2 * N : 4 * N])
        nc.sync.dma_start(n3_sb[:], n3)

        scales_got = keep([P, S], U8, "scales_got")
        nc.vector.tensor_copy(scales_got[:], scales_all[:].indirect(offs_sb[:]))
        x_plane = keep([P, S], U8, "x_plane")
        nc.vector.tensor_copy(x_plane[:].rearrange("p (t m) -> p t m", t=PACK), scales_got[:].rearrange("p (m t) -> p t m", t=PACK))
        x_codes = keep([P, S], U32, "x_codes")
        nc.vector.tensor_copy(x_codes[:].rearrange("p (t m) -> p m t", t=PACK), words_all[:].bitcast(U32).indirect(offs_sb[:]))

        y = [keep([P, H], F32, "y%d" % t) for t in range(PACK)]
        for h in range(2):
            wa_bf = keep([P, HALF, PACK], BF16, "wa_bf%d" % h)
            dst = wa_bf[:].rearrange("p (c i) j -> p c j i", i=4)
            src = wa_raw[h][:].rearrange("p j (c i) -> p c j i", i=4)
            cut = WA_ON_VECTOR[h]
            nc.vector.tensor_copy(dst[:, 0:cut], src[:, 0:cut])
            nc.scalar.copy(dst[:, cut:64], src[:, cut:64])
            wa_codes = keep([P, HALF], U32, "wa_codes%d" % h)
            wa_plane = keep([P, HALF], U8, "wa_plane%d" % h)
            nc.vector.quantize_mx(out=wa_codes[:].bitcast(FP8X4), scales=wa_plane[:], in_=wa_bf[:].rearrange("p n j -> p (n j)"))
            for t in range(PACK):
                bank = psum.tile([P, 512], F32, name="bank%d" % (PACK * h + t))
                nc.tensor.matmul_mx(
                    out=bank[:, 0:HALF],
                    lhsT=x_codes[:, t * P : (t + 1) * P].bitcast(FP8X4),
                    lhsT_scale=x_plane[:, t * P : (t + 1) * P],
                    rhs=wa_codes[:].bitcast(FP8X4),
                    rhs_scale=wa_plane[:],
                    start=True,
                    stop=True,
                )
                nc.scalar.copy(y[t][:, h * HALF : (h + 1) * HALF], bank[:, 0:HALF])

        gt_sign = keep([P, PACK], F32, "gt_sign")
        nc.scalar.activation(gt_sign[:], gt_sb[:], ACT.Sign)
        w1_bf = keep([P, PACK, N], BF16, "w1_bf")
        for j in range(PACK):
            nc.scalar.activation(
                w1_bf[:, j, :].rearrange("p (t m) -> p m t", t=PACK),
                w1_raw[j // 2][:, (j % 2) * N : (j % 2 + 1) * N].rearrange("p (m t) -> p m t", t=PACK),
                ACT.Copy,
                scale=gt_sign[:, j : j + 1],
            )
        w1_codes = [keep([P, P], U32, "w1_codes%d" % t) for t in range(PACK)]
        w1_plane = [keep([P, P], U8, "w1_plane%d" % t) for t in range(PACK)]
        wide = [keep([P, 2 * H], F32, "wide%d" % t) for t in range(PACK)]
        hid = [wide[0][:, H : 2 * H]] + [keep([P, H], F32, "hid%d" % t)[:] for t in range(1, PACK)]
        z_codes = keep([P, H], U32, "z_codes")
        z_plane = keep([P, H], U8, "z_plane")

        z_planes = w1_raw[1][:, N : 2 * N].bitcast(BF16).rearrange("p (t n) -> p t n", t=PACK)

        def less_y(t, c0, c1, part):
            nc.vector.tensor_tensor(part, tab_sb[t][:].indirect(entries(n1_sb, c0, c1)), y[t][:, c0:c1], ALU.subtract)

        def size(t, c0, c1, part, diff):
            nc.vector.tensor_tensor(diff, y[t][:].indirect(entries(n2_sb, c0, c1)), part, ALU.add)
            nc.scalar.activation(z_planes[:, t, :], diff, ACT.Abs, scale=gt_sb[:, t : t + 1])

        def quantise(codes, plane, woven):
            nc.vector.quantize_mx(out=codes.bitcast(FP8X4), scales=plane, in_=woven)

        def second_product(t, c0, c1, bank_name):
            bank = psum.tile([P, 512], F32, name=bank_name)
            nc.tensor.matmul_mx(
                out=bank[:, 0 : c1 - c0],
                lhsT=w1_codes[t][:].bitcast(FP8X4),
                lhsT_scale=w1_plane[t][:],
                rhs=z_codes[:, c0:c1].bitcast(FP8X4),
                rhs_scale=z_plane[:, c0:c1],
                start=True,
                stop=True,
            )
            return bank[:, 0 : c1 - c0]

        def first_tile(c0, c1, bank_name):
            bank = second_product(0, c0, c1, bank_name)
            nc.scalar.activation(sig0[:, c0:c1], bank, ACT.Sigmoid)
            nc.scalar.copy(hid[0][:, c0:c1], bank)

        def by_word(woven):
            return woven.rearrange("p (n t) -> p n t", t=PACK)

        def w1_columns(t):
            return w1_bf[:, :, t * P : (t + 1) * P].rearrange("p j m -> p m j")

        part = [keep([P, HALF if t < 2 else H], F32, "part%d" % t) for t in range(PACK)]
        diff = [keep([P, HALF], F32, "diff%d" % i) for i in range(PACK + 2)]
        less_y(0, 0, HALF, part[0][:])
        less_y(1, 0, HALF, part[1][:])
        size(0, 0, HALF, part[0][:], diff[0][:])
        less_y(2, 0, H, part[2][:])
        size(1, 0, HALF, part[1][:], diff[1][:])
        less_y(3, 0, H, part[3][:])
        size(2, 0, HALF, part[2][:, 0:HALF], diff[2][:])
        size(3, 0, HALF, part[3][:, 0:HALF], diff[3][:])
        z_woven = keep([P, HALF * PACK], BF16, "z_woven0")
        w1_woven = [keep([P, P * PACK], BF16, "w1_woven%d" % t) for t in range(PACK)]
        nc.scalar.copy(by_word(w1_woven[0][:]), w1_columns(0))
        nc.scalar.copy(by_word(z_woven[:]), z_planes.rearrange("p t n -> p n t"))
        for t in range(1, PACK):
            nc.scalar.copy(by_word(w1_woven[t][:]), w1_columns(t))
        quantise(w1_codes[0][:], w1_plane[0][:], w1_woven[0][:])
        quantise(z_codes[:, 0:HALF], z_plane[:, 0:HALF], z_woven[:])
        first_tile(0, HALF, "bank0")

        less_y(0, HALF, H, part[2][:, 0:HALF])
        less_y(1, HALF, H, part[3][:, 0:HALF])
        size(0, HALF, H, part[2][:, 0:HALF], diff[4][:])
        size(1, HALF, H, part[3][:, 0:HALF], diff[5][:])
        spent = z_woven[:].bitcast(F32)
        size(2, HALF, H, part[2][:, HALF:H], spent[:, 0:HALF])
        size(3, HALF, H, part[3][:, HALF:H], spent[:, HALF:H])
        z_woven = keep([P, HALF * PACK], BF16, "z_woven1")
        nc.vector.tensor_copy(by_word(z_woven[:])[:, 0:160, :], z_planes[:, :, 0:160].rearrange("p t n -> p n t"))
        nc.scalar.copy(by_word(z_woven[:])[:, 160:HALF, :], z_planes[:, :, 160:HALF].rearrange("p t n -> p n t"))
        quantise(z_codes[:, HALF:H], z_plane[:, HALF:H], z_woven[:])
        first_tile(HALF, H, "bank4")

        banks = {}
        for t in range(1, PACK):
            quantise(w1_codes[t][:], w1_plane[t][:], w1_woven[t][:])
            banks[t] = second_product(t, 0, H, "bank%d" % t)

        out_rows = out.rearrange("(p t) n -> p t n", t=PACK)
        other = [keep([P, H], F32, "other%d" % t) for t in range(PACK)]
        halves = [(0, HALF), (HALF, H)]

        def gate(t):
            if t == 0:
                for c0, c1 in halves:
                    nc.vector.tensor_tensor(wide[t][:, c0:c1], sig0[:].indirect(entries(n3_sb, c0, c1)), hid[t][:, c0:c1], ALU.mult)
            else:
                nc.scalar.copy(hid[t], banks[t])
                sig = wide[t][:, H : 2 * H]
                for c0, c1 in halves:
                    nc.scalar.activation(sig[:, c0:c1], hid[t].indirect(entries(n3_sb, c0, c1)), ACT.Sigmoid)
                nc.vector.tensor_tensor(wide[t][:, 0:H], hid[t], sig, ALU.mult)

        def fetch(t, c0, c1):
            nc.vector.tensor_copy(other[t][:, c0:c1], wide[t][:].indirect(entries(n3_sb, c0, c1)))

        def larger(t, c0, c1):
            res = keep([P, c1 - c0], F32, "res%d_%d" % (t, c0))
            nc.vector.tensor_tensor(res[:], wide[t][:, c0:c1], other[t][:, c0:c1], ALU.max)
            nc.sync.dma_start(out_rows[:, t, c0:c1], res[:])

        gate(0)
        fetch(0, 0, H)
        gate(1)
        larger(0, 0, H)
        fetch(1, 0, H)
        gate(2)
        larger(1, 0, H)
        fetch(2, 0, H)
        gate(3)
        larger(2, 0, H)
        fetch(3, 0, HALF)
        fetch(3, HALF, H)
        larger(3, 0, HALF)
        larger(3, HALF, H)
